import numpy as np
import ml_dtypes


def mxq(x, axis, fmt="e4m3"):
    dtype, down = {"e4m3": (ml_dtypes.float8_e4m3fn, 7), "e5m2": (ml_dtypes.float8_e5m2, 14)}[fmt]
    v = np.moveaxis(np.asarray(x, np.float32).astype(ml_dtypes.bfloat16).astype(np.float64), axis, -1)
    blocks = v.reshape(v.shape[:-1] + (-1, 32))
    amax = np.abs(blocks).max(-1, keepdims=True)
    byte = np.maximum(np.where(amax > 0, np.frexp(amax)[1] - 1 + 127, 0) - down, 1)
    scale = np.exp2(byte - 127.0)
    codes = (blocks / scale).astype(np.float32).astype(dtype).astype(np.float64)
    return np.moveaxis((codes * scale).reshape(v.shape), -1, axis)


WIDE = False


def mx_kscale(k):
    if not WIDE:
        return np.ones(k)
    levels = np.array([10, -10, 5, -5, 0])
    if k % 512:
        return np.exp2(np.random.permutation(np.resize(levels, k // 32))).repeat(32)
    a = np.empty((k // 512, 16))
    for p in range(k // 512):
        a[p, :8] = np.random.permutation(np.resize(levels, 8))
        for g in range(8):
            far = levels[np.abs(levels - a[p, g]) >= 10]
            a[p, g + 8] = far[np.random.randint(len(far))]
    return np.exp2(a.ravel()).repeat(32)


def f64(x):
    return np.asarray(x).astype(np.float64)


def striped8(idx):
    return np.asarray(idx).reshape(8, -1, 16).transpose(0, 2, 1).reshape(128, -1).astype(np.uint16)


def unstriped8(offs):
    return offs.reshape(8, 16, -1).transpose(0, 2, 1).reshape(8, -1).astype(np.int64)


def pick8(x, idx, run):
    r = np.arange(len(x))
    return x[r[:, None], idx[r % (8 * run) // run]]


E2M1 = np.array([0.0, 0.5, 1.0, 1.5, 2.0, 3.0, 4.0, 6.0, -0.0, -0.5, -1.0, -1.5, -2.0, -3.0, -4.0, -6.0])


def pack_weight(w, fmt):
    k, n = w.shape
    w = f64(np.asarray(w, np.float32).astype(ml_dtypes.bfloat16)).reshape(k // 32, 32, n)
    amax = np.abs(w).max(1)
    if fmt == "e4m3":
        byte = np.frexp(amax)[1] - 1 + 127 - 7
    else:
        mant, ex = np.frexp(amax / 6.0)
        byte = np.where(mant > 0.5, ex, ex - 1) + 127
    byte = np.clip(np.where(amax > 0, byte, 1), 1, 254)
    scaled = (w * np.exp2(127.0 - byte)[:, None, :]).reshape(k, n).astype(np.float32)
    by_word = np.ascontiguousarray(scaled.reshape(k // 512, 128, 4, n).transpose(0, 1, 3, 2))
    if fmt == "e4m3":
        words = by_word.astype(ml_dtypes.float8_e4m3fn).view(np.uint8)
    else:
        c = by_word.astype(ml_dtypes.float4_e2m1fn).view(np.uint8) & 0xF
        words = (c[..., 0::2] | (c[..., 1::2] << 4)).reshape(k // 512, 128, 2 * n)
    return np.ascontiguousarray(words), np.ascontiguousarray(byte.astype(np.uint8).reshape(k // 512, 16, n))


def unpack_weight(words, scales, fmt):
    g, _, n = scales.shape
    words = np.ascontiguousarray(words).reshape(g, 128, n, -1)
    if fmt == "e4m3":
        vals = words.view(ml_dtypes.float8_e4m3fn).astype(np.float64)
    else:
        nib = np.empty((g, 128, n, 4), np.uint8)
        nib[..., 0::2] = words & 0xF
        nib[..., 1::2] = words >> 4
        vals = E2M1[nib]
    vals = vals * np.repeat(np.exp2(scales.astype(np.float64) - 127.0), 8, axis=1)[..., None]
    return vals.transpose(0, 1, 3, 2).reshape(g * 512, n)


D, T, U, X, S, I, Q = 512, 1024, 1024, 1024, 1024, 512, 128


def setup_inputs():
    n = np.random.standard_normal
    idx = np.stack([np.random.permutation(T)[:I] for _ in range(8)])
    idx2 = np.stack([np.random.permutation(U)[:I] for _ in range(8)])
    idx3 = np.stack([np.random.permutation(X)[:I] for _ in range(8)])
    idx4 = np.stack([np.random.permutation(S)[:I] for _ in range(8)])
    idx5 = np.stack([np.random.permutation(S)[:I] for _ in range(8)])
    idx6 = np.stack([np.random.permutation(T)[:I] for _ in range(8)])
    fd = mx_kscale(D)
    keysp = pack_weight(n((D, T)) / fd[:, None], "e2m1")
    notesp = pack_weight(n((D, U)) / fd[:, None], "e4m3")
    usersp = pack_weight(n((D, X)) / fd[:, None], "e2m1")
    shelvesp = pack_weight(n((D, S)) / fd[:, None], "e4m3")
    return {
        "query": (n((D, Q)) * 1.0 / np.sqrt(D) * fd[:, None]).astype(np.float32),
        "keys_words": keysp[0],
        "keys_scales": keysp[1],
        "notes_words": notesp[0],
        "notes_scales": notesp[1],
        "users_words": usersp[0],
        "users_scales": usersp[1],
        "shelves_words": shelvesp[0],
        "shelves_scales": shelvesp[1],
        "offs": striped8(idx),
        "offs2": striped8(idx2),
        "offs3": striped8(idx3),
        "offs4": striped8(idx4),
        "offs5": striped8(idx5),
        "offs6": striped8(idx6),
    }


def reference(query, keys_words, keys_scales, notes_words, notes_scales, users_words, users_scales, shelves_words, shelves_scales, offs, offs2, offs3, offs4, offs5, offs6):
    idx = unstriped8(offs)
    idx2 = unstriped8(offs2)
    idx3 = unstriped8(offs3)
    idx4 = unstriped8(offs4)
    idx5 = unstriped8(offs5)
    idx6 = unstriped8(offs6)
    keysu = unpack_weight(keys_words, keys_scales, "e2m1")
    notesu = unpack_weight(notes_words, notes_scales, "e4m3")
    usersu = unpack_weight(users_words, users_scales, "e2m1")
    shelvesu = unpack_weight(shelves_words, shelves_scales, "e4m3")
    queryq = mxq(f64(query), 0, "e4m3")
    a = queryq.T @ keysu
    b = queryq.T @ notesu
    c0 = queryq.T @ usersu
    d0 = queryq.T @ shelvesu
    hi1 = np.maximum(pick8(a, idx, 16), pick8(b, idx2, 16))
    lo1 = np.minimum(pick8(a, idx, 16), pick8(b, idx2, 16))
    hi2 = np.maximum(pick8(c0, idx3, 16), pick8(d0, idx4, 16))
    lo2 = np.minimum(pick8(c0, idx3, 16), pick8(d0, idx4, 16))
    m1 = np.minimum(hi1, hi2)
    m2 = np.maximum(lo1, lo2)
    f1 = np.zeros((Q, S))
    f1[np.arange(Q)[:, None], idx4[np.arange(Q) % 128 // 16]] = m1
    f2 = np.zeros((Q, T))
    f2[np.arange(Q)[:, None], idx[np.arange(Q) % 128 // 16]] = m2
    dd = d0 - f1
    aa = a + f2
    y = pick8(dd, idx5, 16) + pick8(aa, idx6, 16)
    return y

@@ -1,0 +1,183 @@
+from contextlib import ExitStack
+
+import concourse.mybir as mybir
+
+F32 = mybir.dt.float32
+BF16 = mybir.dt.bfloat16
+I32 = mybir.dt.int32
+U32 = mybir.dt.uint32
+U16 = mybir.dt.uint16
+U8 = mybir.dt.uint8
+FP8X4 = mybir.dt.float8_e4m3fn_x4
+FP4X4 = mybir.dt.float4_e2m1fn_x4
+ALU = mybir.AluOpType
+COPY = mybir.ActivationFunctionType.Copy
+
+P = 128
+Q = 128
+POOL = 1024
+SLOTS = 512
+BANK = 512
+HALF = SLOTS // 2
+FLOPS = 2 * 512 * Q * 4 * POOL
+AA_SPLIT = 672
+
+
+def tile_attend_innertwo_four_kernel(
+    tc, query, keys_words, keys_scales, notes_words, notes_scales, users_words, users_scales,
+    shelves_words, shelves_scales, offs, offs2, offs3, offs4, offs5, offs6, out,
+):
+    nc = tc.nc
+    with ExitStack() as ctx:
+        lists = ctx.enter_context(tc.tile_pool(name="lists", bufs=1))
+        sb = ctx.enter_context(tc.tile_pool(name="sb", bufs=1))
+        psum = ctx.enter_context(tc.psum_pool(name="psum", bufs=1))
+
+        list_in = {"a": offs, "b": offs2, "c": offs3, "d": offs4, "dd": offs5, "aa": offs6}
+        idx = {n: lists.tile([P, SLOTS // 16], U16, name="idx_" + n) for n in list_in}
+
+        def load_list(n):
+            nc.sync.dma_start(idx[n][:], list_in[n])
+
+        def offsets(n, h):
+            return idx[n][:, h * HALF // 16 : (h + 1) * HALF // 16]
+
+        words_in = {"a": keys_words, "b": notes_words, "c": users_words, "d": shelves_words}
+        scales_in = {"a": keys_scales, "b": notes_scales, "c": users_scales, "d": shelves_scales}
+        first_row = {"a": 0, "b": 4, "c": 0, "d": 8}
+        word_bytes = {"a": 2, "b": 4, "c": 2, "d": 4}
+        word_type = {"a": FP4X4, "b": FP8X4, "c": FP4X4, "d": FP8X4}
+        words = {n: sb.tile([P, POOL * word_bytes[n]], U8, name="words_" + n, align_bytes=64) for n in words_in}
+        planes = {n: sb.tile([P, POOL], U8, name="plane_" + n, align_bytes=64) for n in words_in}
+
+        def load_words(n):
+            src = words_in[n][0]
+            if word_bytes[n] == 4:
+                src = src.rearrange("p n t -> p (n t)")
+            nc.sync.dma_start(words[n][:].bitcast(I32), src.bitcast(I32))
+
+        def load_scales(n, quad, queue):
+            row = 32 * quad + first_row[n]
+            queue.dma_start(
+                planes[n][row : row + 4, :].bitcast(I32),
+                scales_in[n][0, 4 * quad : 4 * quad + 4, :].bitcast(I32),
+            )
+
+        for n in ("a", "b", "c"):
+            nc.vector.memset(planes[n][:].bitcast(I32), 0)
+        nc.gpsimd.memset(planes["d"][:].bitcast(I32), 0)
+
+        q_raw = sb.tile([P, 4, Q], F32, name="q_raw")
+        nc.sync.dma_start(q_raw[:], query.rearrange("(p t) q -> p t q", t=4))
+        load_words("a")
+        for quad in range(4):
+            load_scales("a", quad, nc.sync)
+        for quad in range(4):
+            load_scales("d", quad, nc.gpsimd)
+        load_words("b")
+        for quad in range(4):
+            load_scales("b", quad, nc.sync)
+        load_list("a")
+        load_list("b")
+        load_words("d")
+        load_words("c")
+        for quad in range(4):
+            load_scales("c", quad, nc.sync)
+        for n in ("d", "c", "dd", "aa"):
+            load_list(n)
+
+        f1 = sb.tile([P, POOL], F32, name="f1")
+        f2 = sb.tile([P, POOL], F32, name="f2")
+        nc.gpsimd.memset(f1[:], 0.0)
+        nc.gpsimd.memset(f2[:], 0.0)
+
+        q_bf = sb.tile([P, Q, 4], BF16, name="q_bf", align_bytes=64)
+        nc.vector.tensor_copy(
+            q_bf[:].rearrange("p (c i) t -> p c t i", i=4),
+            q_raw[:].rearrange("p t (c i) -> p c t i", i=4),
+        )
+        q_words = sb.tile([P, Q], U32, name="q_words", align_bytes=64)
+        q_plane = sb.tile([P, Q], U8, name="q_plane", align_bytes=64)
+        nc.vector.quantize_mx(
+            out=q_words[:].bitcast(FP8X4), scales=q_plane[:], in_=q_bf[:].rearrange("p q t -> p (q t)")
+        )
+
+        banks = {(n, j): psum.tile([Q, BANK], F32, name="bank_%s%d" % (n, j)) for n in words_in for j in range(2)}
+        score = {n: sb.tile([P, POOL], F32, name="score_" + n) for n in words_in}
+        picked = {(n, h): sb.tile([P, HALF], F32, name="picked_%s%d" % (n, h)) for n in words_in for h in range(2)}
+
+        def scores(n):
+            for j in range(2):
+                wb = word_bytes[n]
+                nc.tensor.matmul_mx(
+                    out=banks[n, j][:],
+                    lhsT=q_words[:].bitcast(FP8X4),
+                    lhsT_scale=q_plane[:],
+                    rhs=words[n][:, j * BANK * wb : (j + 1) * BANK * wb].bitcast(word_type[n]),
+                    rhs_scale=planes[n][first_row[n] : P, j * BANK : (j + 1) * BANK],
+                    start=True,
+                    stop=True,
+                )
+            nc.scalar.activation(score[n][:, 0:BANK], banks[n, 0][:], COPY)
+            nc.vector.tensor_copy(score[n][:, BANK:POOL], banks[n, 1][:])
+
+        def gather_v(n, h):
+            nc.vector.tensor_copy(picked[n, h][:], score[n][:].indirect(offsets(n, h)))
+
+        def gather_s(n, h):
+            nc.scalar.activation(picked[n, h][:], score[n][:].indirect(offsets(n, h)), COPY)
+
+        def pair(name, x, y, op):
+            t = sb.tile([P, HALF], F32, name=name)
+            nc.vector.tensor_tensor(t[:], x[:], y[:], op)
+            return t
+
+        scores("a")
+        gather_v("a", 0)
+        scores("b")
+        gather_s("b", 0)
+        hi1 = {0: pair("hi1_0", picked["a", 0], picked["b", 0], ALU.max)}
+        lo1 = {0: pair("lo1_0", picked["a", 0], picked["b", 0], ALU.min)}
+        scores("d")
+        gather_s("d", 0)
+        scores("c")
+        gather_v("c", 0)
+        for n in ("c", "d", "a", "b"):
+            gather_s(n, 1)
+
+        m2 = sb.tile([P, SLOTS], F32, name="m2")
+        hi2 = {0: pair("hi2_0", picked["c", 0], picked["d", 0], ALU.max)}
+        lo2 = {0: pair("lo2_0", picked["c", 0], picked["d", 0], ALU.min)}
+        m1 = {0: pair("m1_0", hi1[0], hi2[0], ALU.min)}
+        nc.vector.tensor_tensor(m2[:, 0:HALF], lo1[0][:], lo2[0][:], ALU.max)
+        nc.vector.tensor_copy(f1[:].indirect(offsets("d", 0)), m1[0][:])
+
+        hi2[1] = pair("hi2_1", picked["c", 1], picked["d", 1], ALU.max)
+        lo2[1] = pair("lo2_1", picked["c", 1], picked["d", 1], ALU.min)
+        hi1[1] = pair("hi1_1", picked["a", 1], picked["b", 1], ALU.max)
+        lo1[1] = pair("lo1_1", picked["a", 1], picked["b", 1], ALU.min)
+        m1[1] = pair("m1_1", hi1[1], hi2[1], ALU.min)
+        nc.vector.tensor_tensor(m2[:, HALF:SLOTS], lo1[1][:], lo2[1][:], ALU.max)
+        nc.vector.tensor_copy(f1[:].indirect(offsets("d", 1)), m1[1][:])
+        nc.vector.tensor_copy(f2[:].indirect(idx["a"][:]), m2[:])
+
+        dd = sb.tile([P, POOL], F32, name="dd")
+        nc.gpsimd.tensor_tensor(dd[:], score["d"][:], f1[:], ALU.subtract)
+        left = sb.tile([P, SLOTS], F32, name="left")
+        nc.scalar.activation(left[:], dd[:].indirect(idx["dd"][:]), COPY)
+
+        aa = sb.tile([P, POOL], F32, name="aa")
+        nc.vector.tensor_tensor(aa[:, 0:BANK], banks["a", 0][:], f2[:, 0:BANK], ALU.add)
+        nc.vector.tensor_tensor(
+            aa[:, BANK:AA_SPLIT], banks["a", 1][:, 0 : AA_SPLIT - BANK], f2[:, BANK:AA_SPLIT], ALU.add
+        )
+        nc.gpsimd.tensor_tensor(aa[:, AA_SPLIT:POOL], score["a"][:, AA_SPLIT:POOL], f2[:, AA_SPLIT:POOL], ALU.add)
+
+        y0 = sb.tile([P, HALF], F32, name="y0")
+        y1 = sb.tile([P, HALF], F32, name="y1")
+        stands = sb.tile([P, HALF], F32, name="stands")
+        nc.vector.tensor_tensor(y0[:], aa[:].indirect(offsets("aa", 0)), left[:, 0:HALF], ALU.add)
+        nc.scalar.activation(stands[:], aa[:].indirect(offsets("aa", 1)), COPY)
+        nc.sync.dma_start(out[:, 0:HALF], y0[:])
+        nc.vector.tensor_tensor(y1[:], stands[:], left[:, HALF:SLOTS], ALU.add)
+        nc.scalar.dma_start(out[:, HALF:SLOTS], y1[:])

@@ -20,7 +20,7 @@ SLOTS = 512
 BANK = 512
 HALF = SLOTS // 2
 FLOPS = 2 * 512 * Q * 4 * POOL
-AA_SPLIT = 672
+AA_SPLIT = 768
 
 
 def tile_attend_innertwo_four_kernel(
@@ -47,7 +47,10 @@ def tile_attend_innertwo_four_kernel(
         first_row = {"a": 0, "b": 4, "c": 0, "d": 8}
         word_bytes = {"a": 2, "b": 4, "c": 2, "d": 4}
         word_type = {"a": FP4X4, "b": FP8X4, "c": FP4X4, "d": FP8X4}
-        words = {n: sb.tile([P, POOL * word_bytes[n]], U8, name="words_" + n, align_bytes=64) for n in words_in}
+        words = {
+            n: sb.tile([P, POOL * word_bytes[n]], U8, name="words_" + n, tag="words_" + n, align_bytes=64)
+            for n in words_in
+        }
         planes = {n: sb.tile([P, POOL], U8, name="plane_" + n, align_bytes=64) for n in words_in}
 
         def load_words(n):
@@ -75,9 +78,9 @@ def tile_attend_innertwo_four_kernel(
         for quad in range(4):
             load_scales("d", quad, nc.gpsimd)
         load_words("b")
+        load_list("a")
         for quad in range(4):
             load_scales("b", quad, nc.sync)
-        load_list("a")
         load_list("b")
         load_words("d")
         load_words("c")
@@ -85,11 +88,6 @@ def tile_attend_innertwo_four_kernel(
             load_scales("c", quad, nc.sync)
         for n in ("d", "c", "dd", "aa"):
             load_list(n)
-
-        f1 = sb.tile([P, POOL], F32, name="f1")
-        f2 = sb.tile([P, POOL], F32, name="f2")
-        nc.gpsimd.memset(f1[:], 0.0)
-        nc.gpsimd.memset(f2[:], 0.0)
 
         q_bf = sb.tile([P, Q, 4], BF16, name="q_bf", align_bytes=64)
         nc.vector.tensor_copy(
@@ -104,9 +102,9 @@ def tile_attend_innertwo_four_kernel(
 
         banks = {(n, j): psum.tile([Q, BANK], F32, name="bank_%s%d" % (n, j)) for n in words_in for j in range(2)}
         score = {n: sb.tile([P, POOL], F32, name="score_" + n) for n in words_in}
-        picked = {(n, h): sb.tile([P, HALF], F32, name="picked_%s%d" % (n, h)) for n in words_in for h in range(2)}
+        picked = {}
 
-        def scores(n):
+        def scores(n, second):
             for j in range(2):
                 wb = word_bytes[n]
                 nc.tensor.matmul_mx(
@@ -119,46 +117,58 @@ def tile_attend_innertwo_four_kernel(
                     stop=True,
                 )
             nc.scalar.activation(score[n][:, 0:BANK], banks[n, 0][:], COPY)
-            nc.vector.tensor_copy(score[n][:, BANK:POOL], banks[n, 1][:])
+            second(score[n][:, BANK:POOL], banks[n, 1][:])
 
-        def gather_v(n, h):
-            nc.vector.tensor_copy(picked[n, h][:], score[n][:].indirect(offsets(n, h)))
+        def copy_s(dst, src):
+            nc.scalar.activation(dst, src, COPY)
 
-        def gather_s(n, h):
-            nc.scalar.activation(picked[n, h][:], score[n][:].indirect(offsets(n, h)), COPY)
+        def gather(n, h, engine_copy, dst=None):
+            if dst is None:
+                dst = sb.tile([P, HALF], F32, name="picked_%s%d" % (n, h))[:]
+            picked[n, h] = dst
+            engine_copy(dst, score[n][:].indirect(offsets(n, h)))
 
         def pair(name, x, y, op):
             t = sb.tile([P, HALF], F32, name=name)
-            nc.vector.tensor_tensor(t[:], x[:], y[:], op)
-            return t
+            nc.vector.tensor_tensor(t[:], x, y, op)
+            return t[:]
 
-        scores("a")
-        gather_v("a", 0)
-        scores("b")
-        gather_s("b", 0)
+        copy_v = nc.vector.tensor_copy
+        scores("a", copy_v)
+        gather("a", 0, copy_v)
+        scores("b", copy_v)
+        gather("a", 1, copy_s)
+        gather("b", 0, copy_v)
         hi1 = {0: pair("hi1_0", picked["a", 0], picked["b", 0], ALU.max)}
         lo1 = {0: pair("lo1_0", picked["a", 0], picked["b", 0], ALU.min)}
-        scores("d")
-        gather_s("d", 0)
-        scores("c")
-        gather_v("c", 0)
-        for n in ("c", "d", "a", "b"):
-            gather_s(n, 1)
+        f1 = sb.tile([P, POOL], F32, name="f1", tag="words_a", align_bytes=64)
+        f2 = sb.tile([P, POOL], F32, name="f2", tag="words_b", align_bytes=64)
+        nc.gpsimd.memset(f1[:], 0.0)
+        nc.gpsimd.memset(f2[:], 0.0)
+
+        scores("d", copy_s)
+        scores("c", copy_v)
+        gather("c", 0, copy_v)
+        late = sb.tile([P, 3, HALF], F32, name="late", tag="words_c", align_bytes=64)
+        gather("d", 0, copy_s, late[:, 0, :])
+        gather("b", 1, copy_s, late[:, 1, :])
+        gather("c", 1, copy_s)
+        gather("d", 1, copy_s, late[:, 2, :])
 
         m2 = sb.tile([P, SLOTS], F32, name="m2")
         hi2 = {0: pair("hi2_0", picked["c", 0], picked["d", 0], ALU.max)}
         lo2 = {0: pair("lo2_0", picked["c", 0], picked["d", 0], ALU.min)}
         m1 = {0: pair("m1_0", hi1[0], hi2[0], ALU.min)}
-        nc.vector.tensor_tensor(m2[:, 0:HALF], lo1[0][:], lo2[0][:], ALU.max)
-        nc.vector.tensor_copy(f1[:].indirect(offsets("d", 0)), m1[0][:])
+        nc.vector.tensor_tensor(m2[:, 0:HALF], lo1[0], lo2[0], ALU.max)
+        nc.vector.tensor_copy(f1[:].indirect(offsets("d", 0)), m1[0])
 
-        hi2[1] = pair("hi2_1", picked["c", 1], picked["d", 1], ALU.max)
-        lo2[1] = pair("lo2_1", picked["c", 1], picked["d", 1], ALU.min)
         hi1[1] = pair("hi1_1", picked["a", 1], picked["b", 1], ALU.max)
         lo1[1] = pair("lo1_1", picked["a", 1], picked["b", 1], ALU.min)
+        hi2[1] = pair("hi2_1", picked["c", 1], picked["d", 1], ALU.max)
+        lo2[1] = pair("lo2_1", picked["c", 1], picked["d", 1], ALU.min)
         m1[1] = pair("m1_1", hi1[1], hi2[1], ALU.min)
-        nc.vector.tensor_tensor(m2[:, HALF:SLOTS], lo1[1][:], lo2[1][:], ALU.max)
-        nc.vector.tensor_copy(f1[:].indirect(offsets("d", 1)), m1[1][:])
+        nc.vector.tensor_tensor(m2[:, HALF:SLOTS], lo1[1], lo2[1], ALU.max)
+        nc.vector.tensor_copy(f1[:].indirect(offsets("d", 1)), m1[1])
         nc.vector.tensor_copy(f2[:].indirect(idx["a"][:]), m2[:])
 
         dd = sb.tile([P, POOL], F32, name="dd")

from contextlib import ExitStack

import concourse.mybir as mybir

F32 = mybir.dt.float32
BF16 = mybir.dt.bfloat16
I32 = mybir.dt.int32
U32 = mybir.dt.uint32
U16 = mybir.dt.uint16
U8 = mybir.dt.uint8
FP8X4 = mybir.dt.float8_e4m3fn_x4
FP4X4 = mybir.dt.float4_e2m1fn_x4
ALU = mybir.AluOpType
COPY = mybir.ActivationFunctionType.Copy

P = 128
Q = 128
POOL = 1024
SLOTS = 512
BANK = 512
HALF = SLOTS // 2
FLOPS = 2 * 512 * Q * 4 * POOL
AA_SPLIT = 768


def tile_attend_innertwo_four_kernel(
    tc, query, keys_words, keys_scales, notes_words, notes_scales, users_words, users_scales,
    shelves_words, shelves_scales, offs, offs2, offs3, offs4, offs5, offs6, out,
):
    nc = tc.nc
    with ExitStack() as ctx:
        lists = ctx.enter_context(tc.tile_pool(name="lists", bufs=1))
        sb = ctx.enter_context(tc.tile_pool(name="sb", bufs=1))
        psum = ctx.enter_context(tc.psum_pool(name="psum", bufs=1))

        list_in = {"a": offs, "b": offs2, "c": offs3, "d": offs4, "dd": offs5, "aa": offs6}
        idx = {n: lists.tile([P, SLOTS // 16], U16, name="idx_" + n) for n in list_in}

        def load_list(n):
            nc.sync.dma_start(idx[n][:], list_in[n])

        def offsets(n, h):
            return idx[n][:, h * HALF // 16 : (h + 1) * HALF // 16]

        words_in = {"a": keys_words, "b": notes_words, "c": users_words, "d": shelves_words}
        scales_in = {"a": keys_scales, "b": notes_scales, "c": users_scales, "d": shelves_scales}
        first_row = {"a": 0, "b": 4, "c": 0, "d": 8}
        word_bytes = {"a": 2, "b": 4, "c": 2, "d": 4}
        word_type = {"a": FP4X4, "b": FP8X4, "c": FP4X4, "d": FP8X4}
        words = {
            n: sb.tile([P, POOL * word_bytes[n]], U8, name="words_" + n, tag="words_" + n, align_bytes=64)
            for n in words_in
        }
        planes = {n: sb.tile([P, POOL], U8, name="plane_" + n, align_bytes=64) for n in words_in}

        def load_words(n):
            src = words_in[n][0]
            if word_bytes[n] == 4:
                src = src.rearrange("p n t -> p (n t)")
            nc.sync.dma_start(words[n][:].bitcast(I32), src.bitcast(I32))

        def load_scales(n, quad, queue):
            row = 32 * quad + first_row[n]
            queue.dma_start(
                planes[n][row : row + 4, :].bitcast(I32),
                scales_in[n][0, 4 * quad : 4 * quad + 4, :].bitcast(I32),
            )

        for n in ("a", "b", "c"):
            nc.vector.memset(planes[n][:].bitcast(I32), 0)
        nc.gpsimd.memset(planes["d"][:].bitcast(I32), 0)

        q_raw = sb.tile([P, 4, Q], F32, name="q_raw")
        nc.sync.dma_start(q_raw[:], query.rearrange("(p t) q -> p t q", t=4))
        load_words("a")
        for quad in range(4):
            load_scales("a", quad, nc.sync)
        for quad in range(4):
            load_scales("d", quad, nc.gpsimd)
        load_words("b")
        load_list("a")
        for quad in range(4):
            load_scales("b", quad, nc.sync)
        load_list("b")
        load_words("d")
        load_words("c")
        for quad in range(4):
            load_scales("c", quad, nc.sync)
        for n in ("d", "c", "dd", "aa"):
            load_list(n)

        q_bf = sb.tile([P, Q, 4], BF16, name="q_bf", align_bytes=64)
        nc.vector.tensor_copy(
            q_bf[:].rearrange("p (c i) t -> p c t i", i=4),
            q_raw[:].rearrange("p t (c i) -> p c t i", i=4),
        )
        q_words = sb.tile([P, Q], U32, name="q_words", align_bytes=64)
        q_plane = sb.tile([P, Q], U8, name="q_plane", align_bytes=64)
        nc.vector.quantize_mx(
            out=q_words[:].bitcast(FP8X4), scales=q_plane[:], in_=q_bf[:].rearrange("p q t -> p (q t)")
        )

        banks = {(n, j): psum.tile([Q, BANK], F32, name="bank_%s%d" % (n, j)) for n in words_in for j in range(2)}
        score = {n: sb.tile([P, POOL], F32, name="score_" + n) for n in words_in}
        picked = {}

        def scores(n, second):
            for j in range(2):
                wb = word_bytes[n]
                nc.tensor.matmul_mx(
                    out=banks[n, j][:],
                    lhsT=q_words[:].bitcast(FP8X4),
                    lhsT_scale=q_plane[:],
                    rhs=words[n][:, j * BANK * wb : (j + 1) * BANK * wb].bitcast(word_type[n]),
                    rhs_scale=planes[n][first_row[n] : P, j * BANK : (j + 1) * BANK],
                    start=True,
                    stop=True,
                )
            nc.scalar.activation(score[n][:, 0:BANK], banks[n, 0][:], COPY)
            second(score[n][:, BANK:POOL], banks[n, 1][:])

        def copy_s(dst, src):
            nc.scalar.activation(dst, src, COPY)

        def gather(n, h, engine_copy, dst=None):
            if dst is None:
                dst = sb.tile([P, HALF], F32, name="picked_%s%d" % (n, h))[:]
            picked[n, h] = dst
            engine_copy(dst, score[n][:].indirect(offsets(n, h)))

        def pair(name, x, y, op):
            t = sb.tile([P, HALF], F32, name=name)
            nc.vector.tensor_tensor(t[:], x, y, op)
            return t[:]

        copy_v = nc.vector.tensor_copy
        scores("a", copy_v)
        gather("a", 0, copy_v)
        scores("b", copy_v)
        gather("a", 1, copy_s)
        gather("b", 0, copy_v)
        hi1 = {0: pair("hi1_0", picked["a", 0], picked["b", 0], ALU.max)}
        lo1 = {0: pair("lo1_0", picked["a", 0], picked["b", 0], ALU.min)}
        f1 = sb.tile([P, POOL], F32, name="f1", tag="words_a", align_bytes=64)
        f2 = sb.tile([P, POOL], F32, name="f2", tag="words_b", align_bytes=64)
        nc.gpsimd.memset(f1[:], 0.0)
        nc.gpsimd.memset(f2[:], 0.0)

        scores("d", copy_s)
        scores("c", copy_v)
        gather("c", 0, copy_v)
        late = sb.tile([P, 3, HALF], F32, name="late", tag="words_c", align_bytes=64)
        gather("d", 0, copy_s, late[:, 0, :])
        gather("b", 1, copy_s, late[:, 1, :])
        gather("c", 1, copy_s)
        gather("d", 1, copy_s, late[:, 2, :])

        m2 = sb.tile([P, SLOTS], F32, name="m2")
        hi2 = {0: pair("hi2_0", picked["c", 0], picked["d", 0], ALU.max)}
        lo2 = {0: pair("lo2_0", picked["c", 0], picked["d", 0], ALU.min)}
        m1 = {0: pair("m1_0", hi1[0], hi2[0], ALU.min)}
        nc.vector.tensor_tensor(m2[:, 0:HALF], lo1[0], lo2[0], ALU.max)
        nc.vector.tensor_copy(f1[:].indirect(offsets("d", 0)), m1[0])

        hi1[1] = pair("hi1_1", picked["a", 1], picked["b", 1], ALU.max)
        lo1[1] = pair("lo1_1", picked["a", 1], picked["b", 1], ALU.min)
        hi2[1] = pair("hi2_1", picked["c", 1], picked["d", 1], ALU.max)
        lo2[1] = pair("lo2_1", picked["c", 1], picked["d", 1], ALU.min)
        m1[1] = pair("m1_1", hi1[1], hi2[1], ALU.min)
        nc.vector.tensor_tensor(m2[:, HALF:SLOTS], lo1[1], lo2[1], ALU.max)
        nc.vector.tensor_copy(f1[:].indirect(offsets("d", 1)), m1[1])
        nc.vector.tensor_copy(f2[:].indirect(idx["a"][:]), m2[:])

        dd = sb.tile([P, POOL], F32, name="dd")
        nc.gpsimd.tensor_tensor(dd[:], score["d"][:], f1[:], ALU.subtract)
        left = sb.tile([P, SLOTS], F32, name="left")
        nc.scalar.activation(left[:], dd[:].indirect(idx["dd"][:]), COPY)

        aa = sb.tile([P, POOL], F32, name="aa")
        nc.vector.tensor_tensor(aa[:, 0:BANK], banks["a", 0][:], f2[:, 0:BANK], ALU.add)
        nc.vector.tensor_tensor(
            aa[:, BANK:AA_SPLIT], banks["a", 1][:, 0 : AA_SPLIT - BANK], f2[:, BANK:AA_SPLIT], ALU.add
        )
        nc.gpsimd.tensor_tensor(aa[:, AA_SPLIT:POOL], score["a"][:, AA_SPLIT:POOL], f2[:, AA_SPLIT:POOL], ALU.add)

        y0 = sb.tile([P, HALF], F32, name="y0")
        y1 = sb.tile([P, HALF], F32, name="y1")
        stands = sb.tile([P, HALF], F32, name="stands")
        nc.vector.tensor_tensor(y0[:], aa[:].indirect(offsets("aa", 0)), left[:, 0:HALF], ALU.add)
        nc.scalar.activation(stands[:], aa[:].indirect(offsets("aa", 1)), COPY)
        nc.sync.dma_start(out[:, 0:HALF], y0[:])
        nc.vector.tensor_tensor(y1[:], stands[:], left[:, HALF:SLOTS], ALU.add)
        nc.scalar.dma_start(out[:, HALF:SLOTS], y1[:])
